import numpy as np, ml_dtypes
CORES = [100,101,102,103,108,109,110,111]
N = 8
GR, GC = 2, 4
L, KA, KB, F = 4, 1, 2, 128
def setup_inputs(rng):
    return {"a": rng.standard_normal((N, 128, KA * 128), dtype=np.float32).astype(ml_dtypes.bfloat16), "b": rng.standard_normal((N, 128, KB * F), dtype=np.float32).astype(ml_dtypes.bfloat16)}
def setup_inputs_big(rng):
    d = setup_inputs(rng)
    for k in ("a", "b"): d[k] = (d[k].astype(np.float32) * 1024.0).astype(d[k].dtype)
    return d
def setup_inputs_small(rng):
    d = setup_inputs(rng)
    for k in ("a", "b"): d[k] = (d[k].astype(np.float32) * (1 / 1024.0)).astype(d[k].dtype)
    return d
def setup_inputs_apart(rng):
    d = setup_inputs(rng)
    f = (10.0 ** rng.permutation(np.linspace(-1.5, 1.5, N))).astype(np.float32).reshape(N, 1, 1)
    for k in ("a", "b"): d[k] = (d[k].astype(np.float32) * f).astype(d[k].dtype)
    return d
def reference(a, b):
    A, B = a.astype(np.float64), b.astype(np.float64)
    y = np.zeros((N, 128, F))
    for i in range(GR):
        for j in range(GC):
            for k in range(L):
                At = A[i * GC + k // KA][:, 128 * (k % KA):128 * (k % KA) + 128]
                Bt = B[(k // KB) * GC + j][:, F * (k % KB):F * (k % KB) + F]
                y[i * GC + j] += At.T @ Bt
    return {"y": y.astype(ml_dtypes.bfloat16 if a.dtype != np.float64 else np.float64)}

from concourse.bass import DstId, RemoteDMATransfer

GR, GC, KB, F = 2, 4, 2, 128
L = GR * KB

SCRATCH = {
    "A": ("sbuf", [128, L * 128], "bfloat16"),
    "B": ("sbuf", [128, L * F], "bfloat16"),
    "bd": ("dram", [128, KB * F], "bfloat16"),
    "rd": ("dram", [GC, 128, KB * F], "bfloat16"),
    "acc": ("psum", [128, F], "float32"),
    "ysb": ("sbuf", [128, F], "bfloat16"),
}
SEMAPHORES = (["a_ld", "b_ld", "bd_ld", "b_arr", "sent", "mm", "cp", "st"]
              + ["a_arr%d" % k for k in range(GC)] + ["r_arr%d" % k for k in range(GC)])


def _take(mask, n):
    m = 0
    for e in [e for e in range(mask.bit_length()) if (mask >> e) & 1][:n]:
        m |= 1 << e
    return m


def _count(mask):
    return bin(mask).count("1")


def rank_program(g, core, T, topo):
    rank = T.rank_of(core)
    if rank is None:
        return
    row, col = divmod(rank, GC)
    other = 1 - row

    def at(i, j):
        return T.cores[i * GC + j]

    def plan(i):
        own = [j for j in range(GC) if topo.may_write(at(i, j), at(1 - i, j))]
        rest = [j for j in range(GC) if j not in own]
        return own, {j: own[n % len(own)] for n, j in enumerate(rest)}

    def a_mask(i, j):
        mate = at(i, (j + 1) % GC)
        on_chip = topo.mask(at(i, j), mate)
        if j in plan(i)[0]:
            return on_chip & ~topo.mask(at(i, j), at(1 - i, j))
        return _take(on_chip, _count(on_chip) // 2)

    owners, via = plan(row)
    sem = T.sem
    mine = slice(KB * F * row, KB * F * (row + 1))
    a_slot = slice(128 * col, 128 * (col + 1))

    g.sync.dma_start(T.bd[:], T.b[:]).then_inc(sem.bd_ld, 16)
    g.scalar.dma_start(T.A[:, a_slot], T.a[:]).then_inc(sem.a_ld, 16)
    g.scalar.dma_start(T.B[:, mine], T.b[:]).then_inc(sem.b_ld, 16)

    sent = 0
    g.wait_ge(sem.bd_ld, 16)
    if col in owners:
        dst = at(other, col)
        rid, pid, _ = topo.addr(dst)
        m = topo.mask(core, dst)
        g.remote_dma(T.B[:, mine], T.bd[:], sem.b_arr, sem.sent, pid, rid, m)
    else:
        dst = at(row, via[col])
        rid, pid, _ = topo.addr(dst)
        m = _take(topo.mask(core, dst), 4)
        g.remote_dma(T.rd[col], T.bd[:], sem["r_arr%d" % col], sem.sent, pid, rid, m)
    sent += _count(m)

    g.wait_ge(sem.a_ld, 16)
    mates = [at(row, k) for k in range(GC) if k != col]
    m = a_mask(row, col)
    g.remote_dma_fused(
        [RemoteDMATransfer(dst_ids=[DstId(rid=topo.addr(d)[0], pnc=topo.addr(d)[1]) for d in mates],
                           dma_engine_mask=m, remote_sem=sem["a_arr%d" % col],
                           srcs=[T.A[:, a_slot]], dsts=[T.A[:, a_slot] for d in mates], alu_op=0)],
        local_sem=sem.sent)
    sent += _count(m)

    for c in [c for c in via if via[c] == col]:
        src = at(row, c)
        g.wait_ge(sem["r_arr%d" % c], _count(_take(topo.mask(src, core), 4)))
        dst = at(other, c)
        rid, pid, _ = topo.addr(dst)
        m = topo.mask(core, dst)
        g.remote_dma(T.B[:, mine], T.rd[c], sem.b_arr, sem.sent, pid, rid, m)
        sent += _count(m)
    g.wait_ge(sem.sent, sent)

    o_owners, o_via = plan(other)
    b_from = at(other, col if col in o_owners else o_via[col])
    ks = [KB * row + t for t in range(KB)] + [KB * other + t for t in range(KB)]
    g.tensor.wait_ge(sem.b_ld, 16)
    last = None
    for n, k in enumerate(ks):
        if n == KB:
            g.tensor.wait_ge(sem.b_arr, _count(topo.mask(b_from, core)))
        if k == col:
            g.tensor.wait_ge(sem.a_ld, 16)
        else:
            g.tensor.wait_ge(sem["a_arr%d" % k], _count(a_mask(row, k)))
        last = g.tensor.matmul(T.acc[:], T.A[:, 128 * k:128 * (k + 1)], T.B[:, F * k:F * (k + 1)], n == 0, n == L - 1)
    last.then_inc(sem.mm, 1)

    g.vector.wait_ge(sem.mm, 1)
    g.vector.tensor_copy(T.ysb[:], T.acc[:]).then_inc(sem.cp, 1)
    g.sync.wait_ge(sem.cp, 1)
    g.sync.dma_start(T.y[:], T.ysb[:]).then_inc(sem.st, 16)
    g.sync.wait_ge(sem.st, 16)
